import numpy as np
import ml_dtypes


def mxq(x, axis, fmt="e4m3"):
    dtype, down = {"e4m3": (ml_dtypes.float8_e4m3fn, 7), "e5m2": (ml_dtypes.float8_e5m2, 14)}[fmt]
    v = np.moveaxis(np.asarray(x, np.float32).astype(ml_dtypes.bfloat16).astype(np.float64), axis, -1)
    blocks = v.reshape(v.shape[:-1] + (-1, 32))
    amax = np.abs(blocks).max(-1, keepdims=True)
    byte = np.maximum(np.where(amax > 0, np.frexp(amax)[1] - 1 + 127, 0) - down, 1)
    scale = np.exp2(byte - 127.0)
    codes = (blocks / scale).astype(np.float32).astype(dtype).astype(np.float64)
    return np.moveaxis((codes * scale).reshape(v.shape), -1, axis)


WIDE = False


def mx_kscale(k):
    if not WIDE:
        return np.ones(k)
    levels = np.array([10, -10, 5, -5, 0])
    if k % 512:
        return np.exp2(np.random.permutation(np.resize(levels, k // 32))).repeat(32)
    a = np.empty((k // 512, 16))
    for p in range(k // 512):
        a[p, :8] = np.random.permutation(np.resize(levels, 8))
        for g in range(8):
            far = levels[np.abs(levels - a[p, g]) >= 10]
            a[p, g + 8] = far[np.random.randint(len(far))]
    return np.exp2(a.ravel()).repeat(32)


def f64(x):
    return np.asarray(x).astype(np.float64)


def striped(idx):
    return np.tile(np.asarray(idx).reshape(-1, 16).T, (8, 1)).astype(np.uint16)


def unstriped(offs):
    return offs[:16].T.reshape(-1).astype(np.int64)


E2M1 = np.array([0.0, 0.5, 1.0, 1.5, 2.0, 3.0, 4.0, 6.0, -0.0, -0.5, -1.0, -1.5, -2.0, -3.0, -4.0, -6.0])


def pack_weight(w, fmt):
    k, n = w.shape
    w = f64(np.asarray(w, np.float32).astype(ml_dtypes.bfloat16)).reshape(k // 32, 32, n)
    amax = np.abs(w).max(1)
    if fmt == "e4m3":
        byte = np.frexp(amax)[1] - 1 + 127 - 7
    else:
        mant, ex = np.frexp(amax / 6.0)
        byte = np.where(mant > 0.5, ex, ex - 1) + 127
    byte = np.clip(np.where(amax > 0, byte, 1), 1, 254)
    scaled = (w * np.exp2(127.0 - byte)[:, None, :]).reshape(k, n).astype(np.float32)
    by_word = np.ascontiguousarray(scaled.reshape(k // 512, 128, 4, n).transpose(0, 1, 3, 2))
    if fmt == "e4m3":
        words = by_word.astype(ml_dtypes.float8_e4m3fn).view(np.uint8)
    else:
        c = by_word.astype(ml_dtypes.float4_e2m1fn).view(np.uint8) & 0xF
        words = (c[..., 0::2] | (c[..., 1::2] << 4)).reshape(k // 512, 128, 2 * n)
    return np.ascontiguousarray(words), np.ascontiguousarray(byte.astype(np.uint8).reshape(k // 512, 16, n))


def unpack_weight(words, scales, fmt):
    g, _, n = scales.shape
    words = np.ascontiguousarray(words).reshape(g, 128, n, -1)
    if fmt == "e4m3":
        vals = words.view(ml_dtypes.float8_e4m3fn).astype(np.float64)
    else:
        nib = np.empty((g, 128, n, 4), np.uint8)
        nib[..., 0::2] = words & 0xF
        nib[..., 1::2] = words >> 4
        vals = E2M1[nib]
    vals = vals * np.repeat(np.exp2(scales.astype(np.float64) - 127.0), 8, axis=1)[..., None]
    return vals.transpose(0, 1, 3, 2).reshape(g * 512, n)


K, T, J, N = 512, 2048, 512, 512


def setup_inputs():
    n = np.random.standard_normal
    idx = np.random.permutation(T)[:J]
    fk = mx_kscale(K)
    wap = pack_weight(n((K, N)) * 1 / np.sqrt(K) * fk[:, None], "e2m1")
    wbp = pack_weight(n((K, N)) * 1 / np.sqrt(K) * fk[:, None], "e4m3")
    return {
        "xf": (n((K, T))).astype(np.float32),
        "lo": (np.random.uniform(-1.2, -0.4, (K, 1))).astype(np.float32),
        "hi": (np.random.uniform(0.4, 1.2, (K, 1))).astype(np.float32),
        "fa": (np.random.uniform(0.5, 2.0, (K, 1)) / fk[:, None]).astype(np.float32),
        "fb": (np.random.uniform(0.5, 2.0, (K, 1)) / fk[:, None]).astype(np.float32),
        "wa_words": wap[0],
        "wa_scales": wap[1],
        "wb_words": wbp[0],
        "wb_scales": wbp[1],
        "offs": striped(idx),
    }


def reference(xf, lo, hi, fa, fb, wa_words, wa_scales, wb_words, wb_scales, offs):
    idx = unstriped(offs)
    wau = unpack_weight(wa_words, wa_scales, "e2m1")
    wbu = unpack_weight(wb_words, wb_scales, "e4m3")
    b = np.maximum(np.minimum(f64(xf)[:, idx], f64(hi)), f64(lo))
    xa = b * f64(fa)
    xc = (f64(xf)[:, idx] - b) * f64(fb)
    xaq = mxq(xa, 0, "e4m3")
    xcq = mxq(xc, 0, "e4m3")
    y = wau.T @ xaq + wbu.T @ xcq
    return y

@@ -1,0 +1,164 @@
+from contextlib import ExitStack
+
+import concourse.mybir as mybir
+
+K, T, J, N = 512, 2048, 512, 512
+FLOPS = 2 * 2 * K * N * J
+
+F32 = mybir.dt.float32
+BF16 = mybir.dt.bfloat16
+I32 = mybir.dt.int32
+U32 = mybir.dt.uint32
+U16 = mybir.dt.uint16
+U8 = mybir.dt.uint8
+E4M3 = mybir.dt.float8_e4m3fn_x4
+E2M1 = mybir.dt.float4_e2m1fn_x4
+ALU = mybir.AluOpType
+COPY = mybir.ActivationFunctionType.Copy
+
+P = 128
+PACK = 4
+HALF = J // 2
+
+
+def tile_list_bounded_columns_kernel(tc, xf, lo, hi, fa, fb, wa_words, wa_scales, wb_words, wb_scales, offs, out):
+    nc = tc.nc
+    with ExitStack() as ctx:
+        keep = ctx.enter_context(tc.tile_pool(name="keep", bufs=1))
+        psum = ctx.enter_context(tc.psum_pool(name="psum", bufs=1))
+
+        offsets = keep.tile([P, J // 16], U16, name="offsets")
+        planes = [keep.tile([P, T], F32, name=f"plane{t}") for t in range(PACK)]
+        x_rows = xf.rearrange("(p t) c -> p t c", t=PACK)
+        per_k = {}
+        nc.sync.dma_start(out=planes[0][:], in_=x_rows[:, 0, :])
+        nc.sync.dma_start(offsets[:], offs)
+        for name, src in (("hi", hi), ("lo", lo), ("fa", fa), ("fb", fb)):
+            per_k[name] = keep.tile([P, PACK], F32, name=name)
+            nc.scalar.dma_start(out=per_k[name][:], in_=src.rearrange("(p t) o -> p (t o)", t=PACK))
+        for t in range(1, PACK):
+            nc.sync.dma_start(out=planes[t][:], in_=x_rows[:, t, :])
+        wa = keep.tile([P, 2 * N], U8, name="wa", align_bytes=64)
+        wb = keep.tile([P, N], U32, name="wb", align_bytes=64)
+        nc.sync.dma_start(out=wa[:].bitcast(I32), in_=wa_words[0].bitcast(I32))
+        nc.sync.dma_start(out=wb[:].bitcast(I32), in_=wb_words[0].rearrange("p n t -> p (n t)").bitcast(I32))
+        w_scale = []
+        for i, src in enumerate((wa_scales, wb_scales)):
+            sc = keep.tile([P, N], U8, name=f"w_scale{i}", align_bytes=64)
+            nc.gpsimd.memset(sc[:].bitcast(I32), 0)
+            w_scale.append(sc)
+        for sc, src in zip(w_scale, (wa_scales, wb_scales)):
+            for q in range(4):
+                nc.gpsimd.dma_start(out=sc[32 * q : 32 * q + 4, :].bitcast(I32), in_=src[0, 4 * q : 4 * q + 4, :].bitcast(I32))
+
+        picked = [keep.tile([P, J], F32, name=f"picked{t}") for t in range(PACK)]
+        held = [keep.tile([P, J], F32, name=f"held{t}") for t in range(PACK)]
+        cut = [keep.tile([P, J], F32, name=f"cut{t}") for t in range(PACK)]
+        pairs = [keep.tile([P, PACK * J], BF16, name=f"pairs{o}") for o in range(2)]
+        woven = [[keep.tile([P, PACK * HALF], BF16, name=f"woven{o}{h}", align_bytes=64) for h in range(2)] for o in range(2)]
+        codes = [[keep.tile([P, HALF], U32, name=f"codes{o}{h}", align_bytes=64) for h in range(2)] for o in range(2)]
+        scales = [[keep.tile([P, HALF], U8, name=f"scales{o}{h}", align_bytes=64) for h in range(2)] for o in range(2)]
+
+        def cols(h):
+            return slice(0, J) if h is None else slice(h * HALF, (h + 1) * HALF)
+
+        def gather(t, h):
+            c = cols(h)
+            nc.vector.tensor_copy(picked[t][:, c], planes[t][:].indirect(offsets[:, c.start // 16 : c.stop // 16]))
+
+        def clamp(t, h):
+            c = cols(h)
+            nc.vector.tensor_scalar(held[t][:, c], picked[t][:, c], per_k["hi"][:, t : t + 1], per_k["lo"][:, t : t + 1], ALU.min, ALU.max)
+
+        def subtract(t, h):
+            c = cols(h)
+            nc.vector.tensor_tensor(cut[t][:, c], picked[t][:, c], held[t][:, c], ALU.subtract)
+
+        def scale(o, t, h):
+            src = (held, cut)[o][t][:].rearrange("p (h j) -> p h j", h=2)
+            dst = pairs[o][:].rearrange("p (h u j e) -> p h u j e", h=2, u=2, e=2)[:, :, t // 2, :, t % 2]
+            if h is not None:
+                src, dst = src[:, h, :], dst[:, h, :]
+            nc.scalar.activation(dst, src, COPY, scale=per_k[("fa", "fb")[o]][:, t : t + 1])
+
+        def weave(o, h, on_scalar=False):
+            word = U32 if on_scalar else I32
+            src = pairs[o][:, h * PACK * HALF : (h + 1) * PACK * HALF].bitcast(word).rearrange("p (u j) -> p j u", u=2)
+            dst = woven[o][h][:].bitcast(word).rearrange("p (j u) -> p j u", u=2)
+            if on_scalar:
+                nc.scalar.copy(dst, src)
+            else:
+                nc.vector.tensor_copy(dst, src)
+
+        def quantize(o, h):
+            nc.vector.quantize_mx(out=codes[o][h][:].bitcast(E4M3), scales=scales[o][h][:], in_=woven[o][h][:])
+
+        acc = [[psum.tile([P, HALF], F32, name=f"acc{h}{a}") for a in range(N // P)] for h in range(2)]
+
+        def multiply_kept(h):
+            for a in range(N // P):
+                for s in range(HALF // P):
+                    c = slice(s * P, (s + 1) * P)
+                    nc.tensor.matmul_mx(
+                        out=acc[h][a][:, c],
+                        lhsT=wa[:, 2 * P * a : 2 * P * (a + 1)].bitcast(E2M1),
+                        lhsT_scale=w_scale[0][:, P * a : P * (a + 1)],
+                        rhs=codes[0][h][:, c].bitcast(E4M3),
+                        rhs_scale=scales[0][h][:, c],
+                        start=(s == 0),
+                        stop=False,
+                    )
+
+        def multiply_cut(h):
+            for a in range(N // P):
+                nc.tensor.matmul_mx(
+                    out=acc[h][a][:],
+                    lhsT=wb[:, P * a : P * (a + 1)].bitcast(E4M3),
+                    lhsT_scale=w_scale[1][:, P * a : P * (a + 1)],
+                    rhs=codes[1][h][:].bitcast(E4M3),
+                    rhs_scale=scales[1][h][:],
+                    start=False,
+                    stop=True,
+                )
+
+        def store(h):
+            for a in range(N // P):
+                res = keep.tile([P, HALF], F32, name=f"res{h}{a}")
+                if h == 1 and a % 2 == 1:
+                    nc.vector.tensor_copy(res[:], acc[h][a][:])
+                else:
+                    nc.scalar.copy(res[:], acc[h][a][:])
+                nc.sync.dma_start(out=out[P * a : P * (a + 1), cols(h)], in_=res[:])
+
+        for t in range(PACK - 1):
+            gather(t, None)
+            clamp(t, None)
+            scale(0, t, None)
+            subtract(t, None)
+            scale(1, t, None)
+
+        t = PACK - 1
+        gather(t, 0)
+        clamp(t, 0)
+        scale(0, t, 0)
+        gather(t, 1)
+        subtract(t, 0)
+        scale(1, t, 0)
+        weave(0, 0)
+        clamp(t, 1)
+        scale(0, t, 1)
+        quantize(0, 0)
+        multiply_kept(0)
+        weave(0, 1, on_scalar=True)
+        subtract(t, 1)
+        scale(1, t, 1)
+        weave(1, 0)
+        quantize(1, 0)
+        multiply_cut(0)
+        quantize(0, 1)
+        multiply_kept(1)
+        weave(1, 1)
+        quantize(1, 1)
+        multiply_cut(1)
+        store(0)
+        store(1)

@@ -31,25 +31,25 @@ def tile_list_bounded_columns_kernel(tc, xf, lo, hi, fa, fb, wa_words, wa_scales
         planes = [keep.tile([P, T], F32, name=f"plane{t}") for t in range(PACK)]
         x_rows = xf.rearrange("(p t) c -> p t c", t=PACK)
         per_k = {}
-        nc.sync.dma_start(out=planes[0][:], in_=x_rows[:, 0, :])
         nc.sync.dma_start(offsets[:], offs)
-        for name, src in (("hi", hi), ("lo", lo), ("fa", fa), ("fb", fb)):
+        nc.sync.dma_start(out=planes[0][:], in_=x_rows[:, 0, :])
+        for name, src, queue in (("fa", fa, nc.scalar), ("fb", fb, nc.scalar), ("hi", hi, nc.sync), ("lo", lo, nc.sync)):
             per_k[name] = keep.tile([P, PACK], F32, name=name)
-            nc.scalar.dma_start(out=per_k[name][:], in_=src.rearrange("(p t) o -> p (t o)", t=PACK))
+            queue.dma_start(out=per_k[name][:], in_=src.rearrange("(p t) o -> p (t o)", t=PACK))
         for t in range(1, PACK):
             nc.sync.dma_start(out=planes[t][:], in_=x_rows[:, t, :])
         wa = keep.tile([P, 2 * N], U8, name="wa", align_bytes=64)
         wb = keep.tile([P, N], U32, name="wb", align_bytes=64)
-        nc.sync.dma_start(out=wa[:].bitcast(I32), in_=wa_words[0].bitcast(I32))
-        nc.sync.dma_start(out=wb[:].bitcast(I32), in_=wb_words[0].rearrange("p n t -> p (n t)").bitcast(I32))
         w_scale = []
-        for i, src in enumerate((wa_scales, wb_scales)):
+        for i in range(2):
             sc = keep.tile([P, N], U8, name=f"w_scale{i}", align_bytes=64)
             nc.gpsimd.memset(sc[:].bitcast(I32), 0)
             w_scale.append(sc)
-        for sc, src in zip(w_scale, (wa_scales, wb_scales)):
+        for sc, src, queue in zip(w_scale, (wa_scales, wb_scales), (nc.sync, nc.gpsimd)):
             for q in range(4):
-                nc.gpsimd.dma_start(out=sc[32 * q : 32 * q + 4, :].bitcast(I32), in_=src[0, 4 * q : 4 * q + 4, :].bitcast(I32))
+                queue.dma_start(out=sc[32 * q : 32 * q + 4, :].bitcast(I32), in_=src[0, 4 * q : 4 * q + 4, :].bitcast(I32))
+        nc.sync.dma_start(out=wa[:].bitcast(I32), in_=wa_words[0].bitcast(I32))
+        nc.sync.dma_start(out=wb[:].bitcast(I32), in_=wb_words[0].rearrange("p n t -> p (n t)").bitcast(I32))
 
         picked = [keep.tile([P, J], F32, name=f"picked{t}") for t in range(PACK)]
         held = [keep.tile([P, J], F32, name=f"held{t}") for t in range(PACK)]
@@ -124,17 +124,20 @@ def tile_list_bounded_columns_kernel(tc, xf, lo, hi, fa, fb, wa_words, wa_scales
         def store(h):
             for a in range(N // P):
                 res = keep.tile([P, HALF], F32, name=f"res{h}{a}")
-                if h == 1 and a % 2 == 1:
+                if a % 2 == 1:
                     nc.vector.tensor_copy(res[:], acc[h][a][:])
                 else:
                     nc.scalar.copy(res[:], acc[h][a][:])
                 nc.sync.dma_start(out=out[P * a : P * (a + 1), cols(h)], in_=res[:])
 
         for t in range(PACK - 1):
-            gather(t, None)
-            clamp(t, None)
+            gather(t, 0)
+            gather(t, 1)
+            clamp(t, 0)
+            clamp(t, 1)
             scale(0, t, None)
-            subtract(t, None)
+            subtract(t, 0)
+            subtract(t, 1)
             scale(1, t, None)
 
         t = PACK - 1
@@ -144,20 +147,20 @@ def tile_list_bounded_columns_kernel(tc, xf, lo, hi, fa, fb, wa_words, wa_scales
         gather(t, 1)
         subtract(t, 0)
         scale(1, t, 0)
-        weave(0, 0)
         clamp(t, 1)
         scale(0, t, 1)
-        quantize(0, 0)
-        multiply_kept(0)
-        weave(0, 1, on_scalar=True)
+        weave(0, 0)
         subtract(t, 1)
         scale(1, t, 1)
+        quantize(0, 0)
+        multiply_kept(0)
         weave(1, 0)
+        weave(0, 1)
         quantize(1, 0)
         multiply_cut(0)
+        weave(1, 1)
         quantize(0, 1)
         multiply_kept(1)
-        weave(1, 1)
         quantize(1, 1)
         multiply_cut(1)
         store(0)

@@ -45,19 +45,23 @@ def tile_list_bounded_columns_kernel(tc, xf, lo, hi, fa, fb, wa_words, wa_scales
             sc = keep.tile([P, N], U8, name=f"w_scale{i}", align_bytes=64)
             nc.gpsimd.memset(sc[:].bitcast(I32), 0)
             w_scale.append(sc)
-        for sc, src, queue in zip(w_scale, (wa_scales, wb_scales), (nc.sync, nc.gpsimd)):
-            for q in range(4):
-                queue.dma_start(out=sc[32 * q : 32 * q + 4, :].bitcast(I32), in_=src[0, 4 * q : 4 * q + 4, :].bitcast(I32))
         nc.sync.dma_start(out=wa[:].bitcast(I32), in_=wa_words[0].bitcast(I32))
         nc.sync.dma_start(out=wb[:].bitcast(I32), in_=wb_words[0].rearrange("p n t -> p (n t)").bitcast(I32))
+        for q in range(4):
+            for sc, src in zip(w_scale, (wa_scales, wb_scales)):
+                queue = nc.gpsimd if q == 0 else nc.sync
+                queue.dma_start(out=sc[32 * q : 32 * q + 4, :].bitcast(I32), in_=src[0, 4 * q : 4 * q + 4, :].bitcast(I32))
 
         picked = [keep.tile([P, J], F32, name=f"picked{t}") for t in range(PACK)]
         held = [keep.tile([P, J], F32, name=f"held{t}") for t in range(PACK)]
         cut = [keep.tile([P, J], F32, name=f"cut{t}") for t in range(PACK)]
         pairs = [keep.tile([P, PACK * J], BF16, name=f"pairs{o}") for o in range(2)]
-        woven = [[keep.tile([P, PACK * HALF], BF16, name=f"woven{o}{h}", align_bytes=64) for h in range(2)] for o in range(2)]
-        codes = [[keep.tile([P, HALF], U32, name=f"codes{o}{h}", align_bytes=64) for h in range(2)] for o in range(2)]
-        scales = [[keep.tile([P, HALF], U8, name=f"scales{o}{h}", align_bytes=64) for h in range(2)] for o in range(2)]
+        woven2 = [keep.tile([P, 2 * PACK * HALF], BF16, name=f"woven{h}", align_bytes=64) for h in range(2)]
+        codes2 = [keep.tile([P, 2 * HALF], U32, name=f"codes{h}", align_bytes=64) for h in range(2)]
+        scales2 = [keep.tile([P, 2 * HALF], U8, name=f"scales{h}", align_bytes=64) for h in range(2)]
+        woven = [[woven2[h][:, o * PACK * HALF : (o + 1) * PACK * HALF] for h in range(2)] for o in range(2)]
+        codes = [[codes2[h][:, o * HALF : (o + 1) * HALF] for h in range(2)] for o in range(2)]
+        scales = [[scales2[h][:, o * HALF : (o + 1) * HALF] for h in range(2)] for o in range(2)]
 
         def cols(h):
             return slice(0, J) if h is None else slice(h * HALF, (h + 1) * HALF)
@@ -84,19 +88,30 @@ def tile_list_bounded_columns_kernel(tc, xf, lo, hi, fa, fb, wa_words, wa_scales
         def weave(o, h, on_scalar=False):
             word = U32 if on_scalar else I32
             src = pairs[o][:, h * PACK * HALF : (h + 1) * PACK * HALF].bitcast(word).rearrange("p (u j) -> p j u", u=2)
-            dst = woven[o][h][:].bitcast(word).rearrange("p (j u) -> p j u", u=2)
+            dst = woven[o][h].bitcast(word).rearrange("p (j u) -> p j u", u=2)
             if on_scalar:
                 nc.scalar.copy(dst, src)
             else:
                 nc.vector.tensor_copy(dst, src)
 
         def quantize(o, h):
-            nc.vector.quantize_mx(out=codes[o][h][:].bitcast(E4M3), scales=scales[o][h][:], in_=woven[o][h][:])
+            nc.vector.quantize_mx(out=codes[o][h].bitcast(E4M3), scales=scales[o][h], in_=woven[o][h])
 
-        acc = [[psum.tile([P, HALF], F32, name=f"acc{h}{a}") for a in range(N // P)] for h in range(2)]
+        banks = [[psum.tile([P, N], F32, name=f"acc{h}{a}") for a in range(N // P)] for h in range(2)]
+        acc = [[bank[:, :HALF] for bank in row] for row in banks]
+        for bank in acc[0] + acc[1]:
+            nc.tensor.matmul_mx(
+                out=bank[:, :P],
+                lhsT=wb[:, :P].bitcast(E4M3),
+                lhsT_scale=w_scale[1][:, :P],
+                rhs=wb[:, :P].bitcast(E4M3),
+                rhs_scale=w_scale[1][:, :P],
+                start=True,
+                stop=True,
+            )
 
-        def multiply_kept(h):
-            for a in range(N // P):
+        def multiply_kept(h, tiles):
+            for a in tiles:
                 for s in range(HALF // P):
                     c = slice(s * P, (s + 1) * P)
                     nc.tensor.matmul_mx(
@@ -109,14 +124,14 @@ def tile_list_bounded_columns_kernel(tc, xf, lo, hi, fa, fb, wa_words, wa_scales
                         stop=False,
                     )
 
-        def multiply_cut(h):
-            for a in range(N // P):
+        def multiply_cut(h, tiles):
+            for a in tiles:
                 nc.tensor.matmul_mx(
-                    out=acc[h][a][:],
+                    out=acc[h][a],
                     lhsT=wb[:, P * a : P * (a + 1)].bitcast(E4M3),
                     lhsT_scale=w_scale[1][:, P * a : P * (a + 1)],
-                    rhs=codes[1][h][:].bitcast(E4M3),
-                    rhs_scale=scales[1][h][:],
+                    rhs=codes[1][h].bitcast(E4M3),
+                    rhs_scale=scales[1][h],
                     start=False,
                     stop=True,
                 )
@@ -125,9 +140,9 @@ def tile_list_bounded_columns_kernel(tc, xf, lo, hi, fa, fb, wa_words, wa_scales
             for a in range(N // P):
                 res = keep.tile([P, HALF], F32, name=f"res{h}{a}")
                 if a % 2 == 1:
-                    nc.vector.tensor_copy(res[:], acc[h][a][:])
+                    nc.vector.tensor_copy(res[:], acc[h][a])
                 else:
-                    nc.scalar.copy(res[:], acc[h][a][:])
+                    nc.scalar.copy(res[:], acc[h][a])
                 nc.sync.dma_start(out=out[P * a : P * (a + 1), cols(h)], in_=res[:])
 
         for t in range(PACK - 1):
@@ -142,26 +157,26 @@ def tile_list_bounded_columns_kernel(tc, xf, lo, hi, fa, fb, wa_words, wa_scales
 
         t = PACK - 1
         gather(t, 0)
+        gather(t, 1)
         clamp(t, 0)
         scale(0, t, 0)
-        gather(t, 1)
-        subtract(t, 0)
-        scale(1, t, 0)
         clamp(t, 1)
         scale(0, t, 1)
-        weave(0, 0)
+        subtract(t, 0)
+        scale(1, t, 0)
         subtract(t, 1)
         scale(1, t, 1)
+        weave(0, 0)
         quantize(0, 0)
-        multiply_kept(0)
-        weave(1, 0)
+        multiply_kept(0, range(N // P))
         weave(0, 1)
+        weave(1, 0)
         quantize(1, 0)
-        multiply_cut(0)
+        multiply_cut(0, range(N // P))
         weave(1, 1)
-        quantize(0, 1)
-        multiply_kept(1)
-        quantize(1, 1)
-        multiply_cut(1)
+        nc.vector.quantize_mx(out=codes2[1][:].bitcast(E4M3), scales=scales2[1][:], in_=woven2[1][:])
+        for a in range(N // P):
+            multiply_kept(1, [a])
+            multiply_cut(1, [a])
         store(0)
         store(1)

@@ -80,15 +80,14 @@ def tile_list_bounded_columns_kernel(tc, xf, lo, hi, fa, fb, wa_words, wa_scales
 
         def scale(o, t, h):
             src = (held, cut)[o][t][:].rearrange("p (h j) -> p h j", h=2)
-            dst = pairs[o][:].rearrange("p (h u j e) -> p h u j e", h=2, u=2, e=2)[:, :, t // 2, :, t % 2]
+            dst = pairs[o][:].rearrange("p (h t j) -> p h t j", h=2, t=PACK)[:, :, t, :]
             if h is not None:
                 src, dst = src[:, h, :], dst[:, h, :]
             nc.scalar.activation(dst, src, COPY, scale=per_k[("fa", "fb")[o]][:, t : t + 1])
 
         def weave(o, h, on_scalar=False):
-            word = U32 if on_scalar else I32
-            src = pairs[o][:, h * PACK * HALF : (h + 1) * PACK * HALF].bitcast(word).rearrange("p (u j) -> p j u", u=2)
-            dst = woven[o][h].bitcast(word).rearrange("p (j u) -> p j u", u=2)
+            src = pairs[o][:, h * PACK * HALF : (h + 1) * PACK * HALF].rearrange("p (t c i) -> p c t i", t=PACK, i=4)
+            dst = woven[o][h].rearrange("p (c i t) -> p c t i", t=PACK, i=4)
             if on_scalar:
                 nc.scalar.copy(dst, src)
             else:
@@ -110,7 +109,7 @@ def tile_list_bounded_columns_kernel(tc, xf, lo, hi, fa, fb, wa_words, wa_scales
                 stop=True,
             )
 
-        def multiply_kept(h, tiles):
+        def multiply_kept(h, tiles, first):
             for a in tiles:
                 for s in range(HALF // P):
                     c = slice(s * P, (s + 1) * P)
@@ -120,11 +119,11 @@ def tile_list_bounded_columns_kernel(tc, xf, lo, hi, fa, fb, wa_words, wa_scales
                         lhsT_scale=w_scale[0][:, P * a : P * (a + 1)],
                         rhs=codes[0][h][:, c].bitcast(E4M3),
                         rhs_scale=scales[0][h][:, c],
-                        start=(s == 0),
-                        stop=False,
+                        start=(first and s == 0),
+                        stop=(not first and s == HALF // P - 1),
                     )
 
-        def multiply_cut(h, tiles):
+        def multiply_cut(h, tiles, first):
             for a in tiles:
                 nc.tensor.matmul_mx(
                     out=acc[h][a],
@@ -132,14 +131,14 @@ def tile_list_bounded_columns_kernel(tc, xf, lo, hi, fa, fb, wa_words, wa_scales
                     lhsT_scale=w_scale[1][:, P * a : P * (a + 1)],
                     rhs=codes[1][h].bitcast(E4M3),
                     rhs_scale=scales[1][h],
-                    start=False,
-                    stop=True,
+                    start=first,
+                    stop=not first,
                 )
 
         def store(h):
             for a in range(N // P):
                 res = keep.tile([P, HALF], F32, name=f"res{h}{a}")
-                if a % 2 == 1:
+                if h == 1 and a % 2 == 0:
                     nc.vector.tensor_copy(res[:], acc[h][a])
                 else:
                     nc.scalar.copy(res[:], acc[h][a])
@@ -167,16 +166,18 @@ def tile_list_bounded_columns_kernel(tc, xf, lo, hi, fa, fb, wa_words, wa_scales
         subtract(t, 1)
         scale(1, t, 1)
         weave(0, 0)
-        quantize(0, 0)
-        multiply_kept(0, range(N // P))
-        weave(0, 1)
         weave(1, 0)
+        quantize(0, 0)
         quantize(1, 0)
-        multiply_cut(0, range(N // P))
-        weave(1, 1)
-        nc.vector.quantize_mx(out=codes2[1][:].bitcast(E4M3), scales=scales2[1][:], in_=woven2[1][:])
         for a in range(N // P):
-            multiply_kept(1, [a])
-            multiply_cut(1, [a])
+            multiply_kept(0, [a], True)
+            multiply_cut(0, [a], False)
+        weave(1, 1, on_scalar=True)
+        weave(0, 1)
+        quantize(1, 1)
+        quantize(0, 1)
+        for a in range(N // P):
+            multiply_cut(1, [a], True)
+            multiply_kept(1, [a], False)
         store(0)
         store(1)

from contextlib import ExitStack

import concourse.mybir as mybir

K, T, J, N = 512, 2048, 512, 512
FLOPS = 2 * 2 * K * N * J

F32 = mybir.dt.float32
BF16 = mybir.dt.bfloat16
I32 = mybir.dt.int32
U32 = mybir.dt.uint32
U16 = mybir.dt.uint16
U8 = mybir.dt.uint8
E4M3 = mybir.dt.float8_e4m3fn_x4
E2M1 = mybir.dt.float4_e2m1fn_x4
ALU = mybir.AluOpType
COPY = mybir.ActivationFunctionType.Copy

P = 128
PACK = 4
HALF = J // 2


def tile_list_bounded_columns_kernel(tc, xf, lo, hi, fa, fb, wa_words, wa_scales, wb_words, wb_scales, offs, out):
    nc = tc.nc
    with ExitStack() as ctx:
        keep = ctx.enter_context(tc.tile_pool(name="keep", bufs=1))
        psum = ctx.enter_context(tc.psum_pool(name="psum", bufs=1))

        offsets = keep.tile([P, J // 16], U16, name="offsets")
        planes = [keep.tile([P, T], F32, name=f"plane{t}") for t in range(PACK)]
        x_rows = xf.rearrange("(p t) c -> p t c", t=PACK)
        per_k = {}
        nc.sync.dma_start(offsets[:], offs)
        nc.sync.dma_start(out=planes[0][:], in_=x_rows[:, 0, :])
        for name, src, queue in (("fa", fa, nc.scalar), ("fb", fb, nc.scalar), ("hi", hi, nc.sync), ("lo", lo, nc.sync)):
            per_k[name] = keep.tile([P, PACK], F32, name=name)
            queue.dma_start(out=per_k[name][:], in_=src.rearrange("(p t) o -> p (t o)", t=PACK))
        for t in range(1, PACK):
            nc.sync.dma_start(out=planes[t][:], in_=x_rows[:, t, :])
        wa = keep.tile([P, 2 * N], U8, name="wa", align_bytes=64)
        wb = keep.tile([P, N], U32, name="wb", align_bytes=64)
        w_scale = []
        for i in range(2):
            sc = keep.tile([P, N], U8, name=f"w_scale{i}", align_bytes=64)
            nc.gpsimd.memset(sc[:].bitcast(I32), 0)
            w_scale.append(sc)
        nc.sync.dma_start(out=wa[:].bitcast(I32), in_=wa_words[0].bitcast(I32))
        nc.sync.dma_start(out=wb[:].bitcast(I32), in_=wb_words[0].rearrange("p n t -> p (n t)").bitcast(I32))
        for q in range(4):
            for sc, src in zip(w_scale, (wa_scales, wb_scales)):
                queue = nc.gpsimd if q == 0 else nc.sync
                queue.dma_start(out=sc[32 * q : 32 * q + 4, :].bitcast(I32), in_=src[0, 4 * q : 4 * q + 4, :].bitcast(I32))

        picked = [keep.tile([P, J], F32, name=f"picked{t}") for t in range(PACK)]
        held = [keep.tile([P, J], F32, name=f"held{t}") for t in range(PACK)]
        cut = [keep.tile([P, J], F32, name=f"cut{t}") for t in range(PACK)]
        pairs = [keep.tile([P, PACK * J], BF16, name=f"pairs{o}") for o in range(2)]
        woven2 = [keep.tile([P, 2 * PACK * HALF], BF16, name=f"woven{h}", align_bytes=64) for h in range(2)]
        codes2 = [keep.tile([P, 2 * HALF], U32, name=f"codes{h}", align_bytes=64) for h in range(2)]
        scales2 = [keep.tile([P, 2 * HALF], U8, name=f"scales{h}", align_bytes=64) for h in range(2)]
        woven = [[woven2[h][:, o * PACK * HALF : (o + 1) * PACK * HALF] for h in range(2)] for o in range(2)]
        codes = [[codes2[h][:, o * HALF : (o + 1) * HALF] for h in range(2)] for o in range(2)]
        scales = [[scales2[h][:, o * HALF : (o + 1) * HALF] for h in range(2)] for o in range(2)]

        def cols(h):
            return slice(0, J) if h is None else slice(h * HALF, (h + 1) * HALF)

        def gather(t, h):
            c = cols(h)
            nc.vector.tensor_copy(picked[t][:, c], planes[t][:].indirect(offsets[:, c.start // 16 : c.stop // 16]))

        def clamp(t, h):
            c = cols(h)
            nc.vector.tensor_scalar(held[t][:, c], picked[t][:, c], per_k["hi"][:, t : t + 1], per_k["lo"][:, t : t + 1], ALU.min, ALU.max)

        def subtract(t, h):
            c = cols(h)
            nc.vector.tensor_tensor(cut[t][:, c], picked[t][:, c], held[t][:, c], ALU.subtract)

        def scale(o, t, h):
            src = (held, cut)[o][t][:].rearrange("p (h j) -> p h j", h=2)
            dst = pairs[o][:].rearrange("p (h t j) -> p h t j", h=2, t=PACK)[:, :, t, :]
            if h is not None:
                src, dst = src[:, h, :], dst[:, h, :]
            nc.scalar.activation(dst, src, COPY, scale=per_k[("fa", "fb")[o]][:, t : t + 1])

        def weave(o, h, on_scalar=False):
            src = pairs[o][:, h * PACK * HALF : (h + 1) * PACK * HALF].rearrange("p (t c i) -> p c t i", t=PACK, i=4)
            dst = woven[o][h].rearrange("p (c i t) -> p c t i", t=PACK, i=4)
            if on_scalar:
                nc.scalar.copy(dst, src)
            else:
                nc.vector.tensor_copy(dst, src)

        def quantize(o, h):
            nc.vector.quantize_mx(out=codes[o][h].bitcast(E4M3), scales=scales[o][h], in_=woven[o][h])

        banks = [[psum.tile([P, N], F32, name=f"acc{h}{a}") for a in range(N // P)] for h in range(2)]
        acc = [[bank[:, :HALF] for bank in row] for row in banks]
        for bank in acc[0] + acc[1]:
            nc.tensor.matmul_mx(
                out=bank[:, :P],
                lhsT=wb[:, :P].bitcast(E4M3),
                lhsT_scale=w_scale[1][:, :P],
                rhs=wb[:, :P].bitcast(E4M3),
                rhs_scale=w_scale[1][:, :P],
                start=True,
                stop=True,
            )

        def multiply_kept(h, tiles, first):
            for a in tiles:
                for s in range(HALF // P):
                    c = slice(s * P, (s + 1) * P)
                    nc.tensor.matmul_mx(
                        out=acc[h][a][:, c],
                        lhsT=wa[:, 2 * P * a : 2 * P * (a + 1)].bitcast(E2M1),
                        lhsT_scale=w_scale[0][:, P * a : P * (a + 1)],
                        rhs=codes[0][h][:, c].bitcast(E4M3),
                        rhs_scale=scales[0][h][:, c],
                        start=(first and s == 0),
                        stop=(not first and s == HALF // P - 1),
                    )

        def multiply_cut(h, tiles, first):
            for a in tiles:
                nc.tensor.matmul_mx(
                    out=acc[h][a],
                    lhsT=wb[:, P * a : P * (a + 1)].bitcast(E4M3),
                    lhsT_scale=w_scale[1][:, P * a : P * (a + 1)],
                    rhs=codes[1][h].bitcast(E4M3),
                    rhs_scale=scales[1][h],
                    start=first,
                    stop=not first,
                )

        def store(h):
            for a in range(N // P):
                res = keep.tile([P, HALF], F32, name=f"res{h}{a}")
                if h == 1 and a % 2 == 0:
                    nc.vector.tensor_copy(res[:], acc[h][a])
                else:
                    nc.scalar.copy(res[:], acc[h][a])
                nc.sync.dma_start(out=out[P * a : P * (a + 1), cols(h)], in_=res[:])

        for t in range(PACK - 1):
            gather(t, 0)
            gather(t, 1)
            clamp(t, 0)
            clamp(t, 1)
            scale(0, t, None)
            subtract(t, 0)
            subtract(t, 1)
            scale(1, t, None)

        t = PACK - 1
        gather(t, 0)
        gather(t, 1)
        clamp(t, 0)
        scale(0, t, 0)
        clamp(t, 1)
        scale(0, t, 1)
        subtract(t, 0)
        scale(1, t, 0)
        subtract(t, 1)
        scale(1, t, 1)
        weave(0, 0)
        weave(1, 0)
        quantize(0, 0)
        quantize(1, 0)
        for a in range(N // P):
            multiply_kept(0, [a], True)
            multiply_cut(0, [a], False)
        weave(1, 1, on_scalar=True)
        weave(0, 1)
        quantize(1, 1)
        quantize(0, 1)
        for a in range(N // P):
            multiply_cut(1, [a], True)
            multiply_kept(1, [a], False)
        store(0)
        store(1)
